import numpy as np, ml_dtypes
CORES = [24,25,26,27,48,49,50,51,72,73,74,75,96,97,98,99]
N = 16
F = 128
B1, B2, LR, EPS = 0.75, 0.875, 2.0, 0.001
def setup_inputs(rng):
    idle = rng.random((128, N * F)) < 0.125; ib = np.stack([idle[:, F * r:F * r + F] for r in range(N)])
    return {"gr": (rng.standard_normal((N, 128, N * F), dtype=np.float32) * ~idle).astype(ml_dtypes.bfloat16), "m": (rng.standard_normal((N, 128, F), dtype=np.float32) * np.where(ib, 0.004, 1.0)).astype(ml_dtypes.bfloat16), "v": np.where(ib, 2e-6 * 50 ** rng.random((N, 128, F)), (0.5 + rng.standard_normal((N, 128, F), dtype=np.float32) ** 2) * N).astype(ml_dtypes.bfloat16), "w": rng.standard_normal((N, 128, F), dtype=np.float32).astype(ml_dtypes.bfloat16)}
def setup_inputs_big(rng):
    d = setup_inputs(rng)
    for k in ("gr", "m", "v", "w"): d[k] = (d[k].astype(np.float32) * 1024.0).astype(d[k].dtype)
    return d
def setup_inputs_small(rng):
    d = setup_inputs(rng)
    for k in ("gr", "m", "v", "w"): d[k] = (d[k].astype(np.float32) * (1 / 1024.0)).astype(d[k].dtype)
    return d
def setup_inputs_apart(rng):
    d = setup_inputs(rng)
    f = (10.0 ** rng.permutation(np.linspace(-1.5, 1.5, N))).astype(np.float32).reshape(N, 1, 1)
    for k in ("gr", "m", "v", "w"): d[k] = (d[k].astype(np.float32) * f).astype(d[k].dtype)
    return d
def reference(gr, m, v, w):
    GR, M, V, W = gr.astype(np.float64), m.astype(np.float64), v.astype(np.float64), w.astype(np.float64)
    s = GR.sum(axis=0)
    sb = np.stack([s[:, F * r:F * r + F] for r in range(N)])
    m2 = B1 * M + (1 - B1) * sb
    v2 = B2 * V + (1 - B2) * sb ** 2
    w2 = W - LR * m2 / (np.sqrt(v2) + EPS)
    return {"y": np.broadcast_to(np.concatenate(list(w2), axis=1).astype(ml_dtypes.bfloat16), (N, 128, N * F)), "mo": m2.astype(ml_dtypes.bfloat16), "vo": v2.astype(ml_dtypes.bfloat16)}

@@ -1,0 +1,250 @@
+import math
+from concourse.bass import DstId, RemoteDMATransfer
+from concourse.mybir import AluOpType, ActivationFunctionType
+
+N = 16
+F = 128
+B1, B2, LR, EPS = 0.75, 0.875, 2.0, 0.001
+TINY = 1e-12
+
+_BF = "bfloat16"
+_FP = "float32"
+SCRATCH = {
+    "grb": ("sbuf", [128, N * F], _BF),
+    "land": ("sbuf", [128, 3 * 4 * F], _BF),
+    "part": ("sbuf", [128, 4 * F], _BF),
+    "yb": ("sbuf", [128, N * F], _BF),
+    "mb": ("sbuf", [128, F], _BF), "vb": ("sbuf", [128, F], _BF), "wb": ("sbuf", [128, F], _BF),
+    "ones": ("sbuf", [128, F], _BF), "idn": ("sbuf", [128, F], _BF),
+    "i25": ("sbuf", [128, F], _BF), "i75": ("sbuf", [128, F], _BF),
+    "ra": ("sbuf", [128, F], _FP), "ira": ("sbuf", [128, F], _FP), "ia": ("sbuf", [128, F], _FP),
+    "e2": ("sbuf", [128, F], _FP), "n2": ("sbuf", [128, F], _FP), "av": ("sbuf", [128, F], _FP),
+    "dd": ("sbuf", [128, F], _FP), "rec": ("sbuf", [128, F], _FP),
+    "mob": ("sbuf", [128, F], _BF), "vob": ("sbuf", [128, F], _BF),
+    "ps": ("psum", [128, 512], _FP), "pm": ("psum", [128, 512], _FP), "psq": ("psum", [128, 512], _FP),
+    "px": ("psum", [128, 512], _FP), "ph": ("psum", [128, 512], _FP), "pu": ("psum", [128, 512], _FP),
+    "pt": ("psum", [128, 512], _FP),
+}
+SEMAPHORES = (["l0", "l1", "l2", "l3", "lm", "lv", "lw", "s1", "g1", "sent"]
+              + ["p%d" % i for i in range(4)] + ["f%d" % i for i in range(4)] + ["t%d" % i for i in range(4)]
+              + ["tm", "tv", "c_ones", "c_idn", "c_i25", "c_i75", "c_ra", "c_ira", "c_ia", "c_e2", "c_n2", "c_av",
+                 "c_s", "c_m", "c_sq", "c_x", "c_h", "c_um", "c_d", "c_rec", "c_t", "c_w", "c_vo", "c_mo"])
+
+
+def _bits(mask):
+    return [b for b in range(16) if (mask >> b) & 1]
+
+
+def _take(mask, n, i=0):
+    m = 0
+    for b in _bits(mask)[i * n:(i + 1) * n]:
+        m |= 1 << b
+    return m
+
+
+def _count(mask):
+    return len(_bits(mask))
+
+
+def rank_program(g, core, T, topo):
+    rank = T.rank_of(core)
+    if rank is None:
+        return
+    cores = list(T.cores)
+    chips = []
+    for c in cores:
+        if topo.chip(c) not in chips:
+            chips.append(topo.chip(c))
+    members = {ch: [c for c in cores if topo.chip(c) == ch] for ch in chips}
+    W = 4 * F
+
+    def c0(ch):
+        return T.rank_of(members[ch][0]) * F
+
+    def handlers(ch):
+        free = list(members[ch])
+        h = {}
+
+        def cands(b):
+            return [c for c in members[ch] if all(topo.may_write(c, d) for d in members[b])]
+        for b in sorted([b for b in chips if b != ch], key=lambda b: len(cands(b))):
+            c = [x for x in cands(b) if x in free][0]
+            h[b] = c
+            free.remove(c)
+        h[ch] = free[0]
+        return h
+
+    A = topo.chip(core)
+    ciA = chips.index(A)
+    mem = members[A]
+    me = mem.index(core)
+    peers = [c for c in mem if c != core]
+    hA = handlers(A)
+    role = {c: b for b, c in hA.items()}
+    B = role[core]
+    ciB = chips.index(B)
+    sem = T.sem
+    sy, sc, ve, pe = g.sync, g.scalar, g.vector, g.tensor
+    AF, OP = ActivationFunctionType, AluOpType
+    sent = [0]
+
+    def did(c):
+        rid, pid, _ = topo.addr(c)
+        return DstId(rid=rid, pnc=pid)
+
+    targets = [mem[(me + j) % 4] for j in (1, 2, 3)]
+    order = [role[t] for t in targets] + [B]
+    for j, ch in enumerate(order):
+        q = sy if j % 2 == 0 else sc
+        q.dma_start(T.grb[:, c0(ch):c0(ch) + W], T.gr[:, c0(ch):c0(ch) + W]).then_inc(sem["l%d" % j], 16)
+    sc.dma_start(T.vb[:], T.v[:]).then_inc(sem.lv, 16)
+    sy.dma_start(T.mb[:], T.m[:]).then_inc(sem.lm, 16)
+    sy.dma_start(T.wb[:], T.w[:]).then_inc(sem.lw, 16)
+
+    ve.memset(T.ones[:], 1.0).then_inc(sem.c_ones, 1)
+    g.wait_ge(sem.c_ones, 1)
+    g.affine_select(T.idn[:], T.ones[:], [[-1, F]], OP.is_equal, 0.0, 0, 1).then_inc(sem.c_idn, 1)
+    ve.wait_ge(sem.c_idn, 1)
+    ve.tensor_scalar(T.i75[:], T.idn[:], B1, None, OP.mult).then_inc(sem.c_i75, 1)
+    ve.tensor_scalar(T.i25[:], T.idn[:], 1.0 - B1, None, OP.mult).then_inc(sem.c_i25, 1)
+
+    for j, t in enumerate(targets):
+        ch = role[t]
+        slot = [c for c in mem if c != t].index(core)
+        rid, pid, _ = topo.addr(t)
+        mk = topo.mask(core, t)
+        g.wait_ge(sem["l%d" % j], 16)
+        g.remote_dma(T.land[:, slot * W:(slot + 1) * W], T.grb[:, c0(ch):c0(ch) + W], sem.s1, sem.sent, pid, rid, mk)
+        sent[0] += _count(mk)
+    s1_all = sum(_count(topo.mask(p, core)) for p in peers)
+
+    def pieces(k):
+        return [T.grb[:, c0(B) + k * F:c0(B) + (k + 1) * F]] + [T.land[:, s * W + k * F:s * W + (k + 1) * F] for s in range(3)]
+
+    def s2_engines(src, dst_chip):
+        ds = [d for d in members[dst_chip] if d != src]
+        n = _count(topo.mask(src, ds[0])) // len(ds)
+        while 128 % n:
+            n -= 1
+        return n
+    g.wait_ge(sem.l3, 16)
+    g.wait_ge(sem.s1, s1_all)
+    trs = []
+    ne = s2_engines(core, B)
+    for k, d in enumerate(members[B]):
+        if d == core:
+            continue
+        trs.append(RemoteDMATransfer(dst_ids=[did(d)], dma_engine_mask=_take(topo.mask(core, d), ne, len(trs)),
+                                     remote_sem=sem["p%d" % ciA], srcs=pieces(k),
+                                     dsts=[T.part[:, ciA * F:(ciA + 1) * F]], alu_op=1))
+        sent[0] += ne
+    g.remote_dma_fused(trs, local_sem=sem.sent)
+
+    sc.wait_ge(sem.lv, 16)
+    sc.activation(T.ra[:], T.vb[:], AF.Sqrt, bias=TINY, scale=B2).then_inc(sem.c_ra, 1)
+    sc.activation(T.av[:], T.vb[:], AF.Copy, scale=B2).then_inc(sem.c_av, 1)
+    ve.wait_ge(sem.c_ra, 1)
+    ve.reciprocal(T.ira[:], T.ra[:]).then_inc(sem.c_ira, 1)
+    ve.wait_ge(sem.c_ira, 1)
+    ve.tensor_tensor(T.ia[:], T.ira[:], T.ira[:], OP.mult).then_inc(sem.c_ia, 1)
+    ve.tensor_scalar(T.e2[:], T.ira[:], EPS, None, OP.mult).then_inc(sem.c_e2, 1)
+    ve.tensor_scalar(T.n2[:], T.ira[:], -LR, None, OP.mult).then_inc(sem.c_n2, 1)
+
+    ps, pm = T.ps[:, 0:F], T.pm[:, 0:F]
+    todo = []
+    if B == A:
+        raw = pieces(me)
+        todo.append((sem.l3, 16, raw[0]))
+        for r in raw[1:]:
+            todo.append((sem.s1, s1_all, r))
+    else:
+        todo.append((sem["p%d" % ciA], s2_engines(hA[A], A), T.part[:, ciA * F:(ciA + 1) * F]))
+    away = sorted([b for b in chips if b != A], key=lambda b: 0 if topo.same_plane(A, b) else 1)
+    for b in away:
+        ci = chips.index(b)
+        todo.append((sem["p%d" % ci], s2_engines(handlers(b)[A], A), T.part[:, ci * F:(ci + 1) * F]))
+    pe.wait_ge(sem.c_idn, 1)
+    pe.wait_ge(sem.c_i75, 1)
+    pe.wait_ge(sem.c_i25, 1)
+    pe.wait_ge(sem.lm, 16)
+    pe.matmul(pm, T.i75[:], T.mb[:], True, False)
+    for i, (s, n, ap) in enumerate(todo):
+        last = i == len(todo) - 1
+        pe.wait_ge(s, n)
+        a = pe.matmul(ps, T.idn[:], ap, i == 0, last)
+        if last:
+            a.then_inc(sem.c_s, 1)
+        b_ = pe.matmul(pm, T.i25[:], ap, False, last)
+        if last:
+            b_.then_inc(sem.c_m, 1)
+
+    own = T.yb[:, rank * F:(rank + 1) * F]
+    psq, px, ph, pu, pt = T.psq[:, 0:F], T.px[:, 0:F], T.ph[:, 0:F], T.pu[:, 0:F], T.pt[:, 0:F]
+    sc.wait_ge(sem.c_s, 1)
+    sc.activation(psq, ps, AF.Square, scale=math.sqrt(1.0 - B2)).then_inc(sem.c_sq, 1)
+    ve.wait_ge(sem.c_ia, 1)
+    ve.wait_ge(sem.c_sq, 1)
+    ve.tensor_tensor(px, psq, T.ia[:], OP.mult).then_inc(sem.c_x, 1)
+    sc.wait_ge(sem.c_x, 1)
+    sc.activation(ph, px, AF.Sqrt, bias=1.0, scale=1.0).then_inc(sem.c_h, 1)
+    ve.wait_ge(sem.c_n2, 1)
+    ve.wait_ge(sem.c_m, 1)
+    ve.tensor_tensor(pu, pm, T.n2[:], OP.mult).then_inc(sem.c_um, 1)
+    ve.wait_ge(sem.c_av, 1)
+    ve.tensor_tensor(T.vob[:], psq, T.av[:], OP.add).then_inc(sem.c_vo, 1)
+    ve.wait_ge(sem.c_e2, 1)
+    ve.wait_ge(sem.c_h, 1)
+    ve.tensor_tensor(T.dd[:], ph, T.e2[:], OP.add).then_inc(sem.c_d, 1)
+    ve.wait_ge(sem.c_d, 1)
+    ve.reciprocal(T.rec[:], T.dd[:]).then_inc(sem.c_rec, 1)
+    ve.wait_ge(sem.c_rec, 1)
+    ve.wait_ge(sem.c_um, 1)
+    ve.tensor_tensor(pt, pu, T.rec[:], OP.mult).then_inc(sem.c_t, 1)
+    ve.wait_ge(sem.c_t, 1)
+    ve.wait_ge(sem.lw, 16)
+    ve.tensor_tensor(own, pt, T.wb[:], OP.add).then_inc(sem.c_w, 1)
+    sc.wait_ge(sem.c_um, 1)
+    sc.activation(T.mob[:], pm, AF.Copy).then_inc(sem.c_mo, 1)
+    sy.wait_ge(sem.c_vo, 1)
+    sy.dma_start(T.vo[:], T.vob[:]).then_inc(sem.tv, 16)
+    sc.wait_ge(sem.c_mo, 1)
+    sc.dma_start(T.mo[:], T.mob[:]).then_inc(sem.tm, 16)
+
+    def to_peers(ap, rsem):
+        mk = topo.mask(core, peers[0])
+        for p in peers:
+            mk &= topo.mask(core, p)
+        g.remote_dma_fused([RemoteDMATransfer(dst_ids=[did(p) for p in peers], dma_engine_mask=mk, remote_sem=rsem,
+                                              srcs=[ap], dsts=[ap for p in peers], alu_op=0)], local_sem=sem.sent)
+        sent[0] += _count(mk)
+    g.wait_ge(sem.c_w, 1)
+    to_peers(own, sem.g1)
+    g1_all = sum(_count(topo.mask(p, core)) for p in peers)
+
+    chunkA = T.yb[:, c0(A):c0(A) + W]
+    if B != A:
+        partner = handlers(B)[A]
+        rid, pid, _ = topo.addr(partner)
+        mk = topo.mask(core, partner)
+        g.wait_ge(sem.g1, g1_all)
+        g.remote_dma(chunkA, chunkA, sem["f%d" % ciA], sem.sent, pid, rid, mk)
+        sent[0] += _count(mk)
+        g.wait_ge(sem["f%d" % ciB], _count(topo.mask(partner, core)))
+        to_peers(T.yb[:, c0(B):c0(B) + W], sem["f%d" % ciB])
+
+    sy.wait_ge(sem.c_w, 1)
+    sy.wait_ge(sem.g1, g1_all)
+    sy.dma_start(T.y[:, c0(A):c0(A) + W], chunkA).then_inc(sem["t%d" % ciA], 16)
+    rest = ([B] if B != A else []) + [b for b in away if b != B]
+    for i, b in enumerate(rest):
+        ci = chips.index(b)
+        src = handlers(b)[A] if b == B else hA[b]
+        q = sc if i % 2 == 0 else sy
+        q.wait_ge(sem["f%d" % ci], _count(topo.mask(src, core)))
+        q.dma_start(T.y[:, c0(b):c0(b) + W], T.yb[:, c0(b):c0(b) + W]).then_inc(sem["t%d" % ci], 16)
+
+    g.wait_ge(sem.sent, sent[0])
+    g.wait_ge(sem.tm, 16)
+    g.wait_ge(sem.tv, 16)
+    for ci in range(4):
+        g.wait_ge(sem["t%d" % ci], 16)

@@ -25,8 +25,9 @@ SCRATCH = {
     "px": ("psum", [128, 512], _FP), "ph": ("psum", [128, 512], _FP), "pu": ("psum", [128, 512], _FP),
     "pt": ("psum", [128, 512], _FP),
 }
-SEMAPHORES = (["l0", "l1", "l2", "l3", "lm", "lv", "lw", "s1", "g1", "sent"]
-              + ["p%d" % i for i in range(4)] + ["f%d" % i for i in range(4)] + ["t%d" % i for i in range(4)]
+SEMAPHORES = (["l0", "l1", "l2", "l3", "lm", "lv", "lw", "s1", "sent"]
+              + ["p%d" % i for i in range(4)] + ["q%d" % i for i in range(4)] + ["e%d" % i for i in range(4)]
+              + ["f%d" % i for i in range(4)] + ["t%d" % i for i in range(8)]
               + ["tm", "tv", "c_ones", "c_idn", "c_i25", "c_i75", "c_ra", "c_ira", "c_ia", "c_e2", "c_n2", "c_av",
                  "c_s", "c_m", "c_sq", "c_x", "c_h", "c_um", "c_d", "c_rec", "c_t", "c_w", "c_vo", "c_mo"])
 
@@ -46,6 +47,16 @@ def _count(mask):
     return len(_bits(mask))
 
 
+def _runs(ks):
+    out = []
+    for k in sorted(ks):
+        if out and out[-1][1] == k:
+            out[-1] = (out[-1][0], k + 1)
+        else:
+            out.append((k, k + 1))
+    return out
+
+
 def rank_program(g, core, T, topo):
     rank = T.rank_of(core)
     if rank is None:
@@ -61,12 +72,15 @@ def rank_program(g, core, T, topo):
     def c0(ch):
         return T.rank_of(members[ch][0]) * F
 
+    def direct(o, ch):
+        return all(topo.may_write(o, d) for d in members[ch])
+
     def handlers(ch):
         free = list(members[ch])
         h = {}
 
         def cands(b):
-            return [c for c in members[ch] if all(topo.may_write(c, d) for d in members[b])]
+            return [c for c in members[ch] if direct(c, b)]
         for b in sorted([b for b in chips if b != ch], key=lambda b: len(cands(b))):
             c = [x for x in cands(b) if x in free][0]
             h[b] = c
@@ -108,37 +122,52 @@ def rank_program(g, core, T, topo):
     ve.tensor_scalar(T.i75[:], T.idn[:], B1, None, OP.mult).then_inc(sem.c_i75, 1)
     ve.tensor_scalar(T.i25[:], T.idn[:], 1.0 - B1, None, OP.mult).then_inc(sem.c_i25, 1)
 
+    def s1_mask(src, dst):
+        j = (mem.index(dst) - mem.index(src) - 1) % 4
+        full = topo.mask(src, dst)
+        return full if j == 2 else _take(full, _count(full) // 2, j)
     for j, t in enumerate(targets):
         ch = role[t]
         slot = [c for c in mem if c != t].index(core)
         rid, pid, _ = topo.addr(t)
-        mk = topo.mask(core, t)
+        mk = s1_mask(core, t)
         g.wait_ge(sem["l%d" % j], 16)
         g.remote_dma(T.land[:, slot * W:(slot + 1) * W], T.grb[:, c0(ch):c0(ch) + W], sem.s1, sem.sent, pid, rid, mk)
         sent[0] += _count(mk)
-    s1_all = sum(_count(topo.mask(p, core)) for p in peers)
+    s1_all = sum(_count(s1_mask(p, core)) for p in peers)
 
     def pieces(k):
         return [T.grb[:, c0(B) + k * F:c0(B) + (k + 1) * F]] + [T.land[:, s * W + k * F:s * W + (k + 1) * F] for s in range(3)]
 
-    def s2_engines(src, dst_chip):
-        ds = [d for d in members[dst_chip] if d != src]
-        n = _count(topo.mask(src, ds[0])) // len(ds)
+    def s2_groups(src, dch):
+        ds = [(k, d) for k, d in enumerate(members[dch]) if d != src]
+        if topo.chip(src) == dch:
+            return [ds]
+        need = [x for x in ds if not all(direct(x[1], z) for z in chips if z != dch)]
+        rest = [x for x in ds if x not in need]
+        return [gp for gp in (need, rest) if gp]
+
+    def s2_ne(src, gp):
+        n = _count(topo.mask(src, gp[0][1])) // len(gp)
         while 128 % n:
             n -= 1
         return n
+
+    def s2_inc(src, dst):
+        for gp in s2_groups(src, topo.chip(dst)):
+            if dst in [d for k, d in gp]:
+                return s2_ne(src, gp)
     g.wait_ge(sem.l3, 16)
     g.wait_ge(sem.s1, s1_all)
-    trs = []
-    ne = s2_engines(core, B)
-    for k, d in enumerate(members[B]):
-        if d == core:
-            continue
-        trs.append(RemoteDMATransfer(dst_ids=[did(d)], dma_engine_mask=_take(topo.mask(core, d), ne, len(trs)),
-                                     remote_sem=sem["p%d" % ciA], srcs=pieces(k),
-                                     dsts=[T.part[:, ciA * F:(ciA + 1) * F]], alu_op=1))
-        sent[0] += ne
-    g.remote_dma_fused(trs, local_sem=sem.sent)
+    for gp in s2_groups(core, B):
+        ne = s2_ne(core, gp)
+        trs = []
+        for k, d in gp:
+            trs.append(RemoteDMATransfer(dst_ids=[did(d)], dma_engine_mask=_take(topo.mask(core, d), ne, len(trs)),
+                                         remote_sem=sem["p%d" % ciA], srcs=pieces(k),
+                                         dsts=[T.part[:, ciA * F:(ciA + 1) * F]], alu_op=1))
+            sent[0] += ne
+        g.remote_dma_fused(trs, local_sem=sem.sent)
 
     sc.wait_ge(sem.lv, 16)
     sc.activation(T.ra[:], T.vb[:], AF.Sqrt, bias=TINY, scale=B2).then_inc(sem.c_ra, 1)
@@ -158,11 +187,11 @@ def rank_program(g, core, T, topo):
         for r in raw[1:]:
             todo.append((sem.s1, s1_all, r))
     else:
-        todo.append((sem["p%d" % ciA], s2_engines(hA[A], A), T.part[:, ciA * F:(ciA + 1) * F]))
+        todo.append((sem["p%d" % ciA], s2_inc(hA[A], core), T.part[:, ciA * F:(ciA + 1) * F]))
     away = sorted([b for b in chips if b != A], key=lambda b: 0 if topo.same_plane(A, b) else 1)
     for b in away:
         ci = chips.index(b)
-        todo.append((sem["p%d" % ci], s2_engines(handlers(b)[A], A), T.part[:, ci * F:(ci + 1) * F]))
+        todo.append((sem["p%d" % ci], s2_inc(handlers(b)[A], core), T.part[:, ci * F:(ci + 1) * F]))
     pe.wait_ge(sem.c_idn, 1)
     pe.wait_ge(sem.c_i75, 1)
     pe.wait_ge(sem.c_i25, 1)
@@ -190,8 +219,6 @@ def rank_program(g, core, T, topo):
     ve.wait_ge(sem.c_n2, 1)
     ve.wait_ge(sem.c_m, 1)
     ve.tensor_tensor(pu, pm, T.n2[:], OP.mult).then_inc(sem.c_um, 1)
-    ve.wait_ge(sem.c_av, 1)
-    ve.tensor_tensor(T.vob[:], psq, T.av[:], OP.add).then_inc(sem.c_vo, 1)
     ve.wait_ge(sem.c_e2, 1)
     ve.wait_ge(sem.c_h, 1)
     ve.tensor_tensor(T.dd[:], ph, T.e2[:], OP.add).then_inc(sem.c_d, 1)
@@ -203,6 +230,8 @@ def rank_program(g, core, T, topo):
     ve.wait_ge(sem.c_t, 1)
     ve.wait_ge(sem.lw, 16)
     ve.tensor_tensor(own, pt, T.wb[:], OP.add).then_inc(sem.c_w, 1)
+    ve.wait_ge(sem.c_av, 1)
+    ve.tensor_tensor(T.vob[:], psq, T.av[:], OP.add).then_inc(sem.c_vo, 1)
     sc.wait_ge(sem.c_um, 1)
     sc.activation(T.mob[:], pm, AF.Copy).then_inc(sem.c_mo, 1)
     sy.wait_ge(sem.c_vo, 1)
@@ -210,41 +239,88 @@ def rank_program(g, core, T, topo):
     sc.wait_ge(sem.c_mo, 1)
     sc.dma_start(T.mo[:], T.mob[:]).then_inc(sem.tm, 16)
 
-    def to_peers(ap, rsem):
-        mk = topo.mask(core, peers[0])
-        for p in peers:
-            mk &= topo.mask(core, p)
-        g.remote_dma_fused([RemoteDMATransfer(dst_ids=[did(p) for p in peers], dma_engine_mask=mk, remote_sem=rsem,
-                                              srcs=[ap], dsts=[ap for p in peers], alu_op=0)], local_sem=sem.sent)
+    def spread(ap, dsts, rsem):
+        mk = topo.mask(core, dsts[0])
+        for d in dsts:
+            mk &= topo.mask(core, d)
+        g.remote_dma_fused([RemoteDMATransfer(dst_ids=[did(d) for d in dsts], dma_engine_mask=mk, remote_sem=rsem,
+                                              srcs=[ap], dsts=[ap for d in dsts], alu_op=0)], local_sem=sem.sent)
         sent[0] += _count(mk)
-    g.wait_ge(sem.c_w, 1)
-    to_peers(own, sem.g1)
-    g1_all = sum(_count(topo.mask(p, core)) for p in peers)
 
-    chunkA = T.yb[:, c0(A):c0(A) + W]
+    def cols(ch, run):
+        return slice(c0(ch) + run[0] * F, c0(ch) + run[1] * F)
+
+    def dset(x, y):
+        d = [k for k, o in enumerate(members[x]) if direct(o, y)]
+        return d, [k for k in range(len(members[x])) if k not in d]
+
+    on_n = _count(topo.mask(core, peers[0]))
+
+    def off_mask(c):
+        mk = topo.mask(c, [p for p in mem if p != c][0])
+        for z in chips:
+            if z != A and direct(c, z):
+                mk &= topo.mask(c, handlers(z)[A])
+        return mk
+
+    def duty(c):
+        return role[c] != A and len(dset(A, role[c])[1]) > 0
+
+    def g1_n(k):
+        return on_n - _count(off_mask(mem[k])) if duty(mem[k]) else on_n
+    far_dsts = [handlers(z)[A] for z in chips if z != A and direct(core, z)]
+    g.wait_ge(sem.c_w, 1)
+    if duty(core):
+        mo_ = off_mask(core)
+        mi_ = topo.mask(core, peers[0]) & ~mo_
+        g.remote_dma_fused([
+            RemoteDMATransfer(dst_ids=[did(d) for d in far_dsts], dma_engine_mask=mo_, remote_sem=sem["e%d" % ciA],
+                              srcs=[own], dsts=[own for d in far_dsts], alu_op=0),
+            RemoteDMATransfer(dst_ids=[did(d) for d in peers], dma_engine_mask=mi_, remote_sem=sem["q%d" % me],
+                              srcs=[own], dsts=[own for d in peers], alu_op=0)], local_sem=sem.sent)
+        sent[0] += _count(mo_) + _count(mi_)
+    else:
+        spread(own, peers, sem["q%d" % me])
+        spread(own, far_dsts, sem["e%d" % ciA])
     if B != A:
         partner = handlers(B)[A]
-        rid, pid, _ = topo.addr(partner)
-        mk = topo.mask(core, partner)
-        g.wait_ge(sem.g1, g1_all)
-        g.remote_dma(chunkA, chunkA, sem["f%d" % ciA], sem.sent, pid, rid, mk)
-        sent[0] += _count(mk)
-        g.wait_ge(sem["f%d" % ciB], _count(topo.mask(partner, core)))
-        to_peers(T.yb[:, c0(B):c0(B) + W], sem["f%d" % ciB])
+        off_n = _count(topo.mask(partner, core))
+        rel = dset(A, B)[1]
+        for k in rel:
+            g.wait_ge(sem["q%d" % k], g1_n(k))
+        for run in _runs(rel):
+            spread(T.yb[:, cols(A, run)], [partner], sem["f%d" % ciA])
+        dB, rB = dset(B, A)
+        g.wait_ge(sem["e%d" % ciB], off_n * len(dB))
+        for run in _runs(dB):
+            spread(T.yb[:, cols(B, run)], peers, sem["e%d" % ciB])
+        if rB:
+            g.wait_ge(sem["f%d" % ciB], off_n * len(_runs(rB)))
+            for run in _runs(rB):
+                spread(T.yb[:, cols(B, run)], peers, sem["f%d" % ciB])
 
-    sy.wait_ge(sem.c_w, 1)
-    sy.wait_ge(sem.g1, g1_all)
-    sy.dma_start(T.y[:, c0(A):c0(A) + W], chunkA).then_inc(sem["t%d" % ciA], 16)
-    rest = ([B] if B != A else []) + [b for b in away if b != B]
-    for i, b in enumerate(rest):
-        ci = chips.index(b)
-        src = handlers(b)[A] if b == B else hA[b]
-        q = sc if i % 2 == 0 else sy
-        q.wait_ge(sem["f%d" % ci], _count(topo.mask(src, core)))
-        q.dma_start(T.y[:, c0(b):c0(b) + W], T.yb[:, c0(b):c0(b) + W]).then_inc(sem["t%d" % ci], 16)
+    jobs = [([(sem.c_w, 1)] + [(sem["q%d" % k], g1_n(k)) for k in range(4) if k != me], slice(c0(A), c0(A) + W))]
+    first = ([B] if B != A else []) + [b for b in away if b != B]
+    for part in (0, 1):
+        for b in first:
+            ci = chips.index(b)
+            ks = dset(b, A)[part]
+            if not ks:
+                continue
+            if b == B:
+                n = _count(topo.mask(handlers(b)[A], core)) * (len(ks) if part == 0 else len(_runs(ks)))
+            else:
+                n = on_n * len(_runs(ks))
+            for run in _runs(ks):
+                jobs.append(([(sem[("e%d" if part == 0 else "f%d") % ci], n)], cols(b, run)))
+    for i, (ws, cs) in enumerate(jobs):
+        q = sy if i % 2 == 0 else sc
+        for s, n in ws:
+            q.wait_ge(s, n)
+        q.dma_start(T.y[:, cs], T.yb[:, cs]).then_inc(sem["t%d" % i], 16)
 
     g.wait_ge(sem.sent, sent[0])
     g.wait_ge(sem.tm, 16)
     g.wait_ge(sem.tv, 16)
-    for ci in range(4):
-        g.wait_ge(sem["t%d" % ci], 16)
+    for i in range(len(jobs)):
+        g.wait_ge(sem["t%d" % i], 16)

@@ -4,6 +4,7 @@ from concourse.mybir import AluOpType, ActivationFunctionType
 
 N = 16
 F = 128
+SIMULATED = 112
 B1, B2, LR, EPS = 0.75, 0.875, 2.0, 0.001
 TINY = 1e-12
 
@@ -11,7 +12,7 @@ _BF = "bfloat16"
 _FP = "float32"
 SCRATCH = {
     "grb": ("sbuf", [128, N * F], _BF),
-    "land": ("sbuf", [128, 3 * 4 * F], _BF),
+    "land": ("sbuf", [128, 4 * 4 * F], _BF),
     "part": ("sbuf", [128, 4 * F], _BF),
     "yb": ("sbuf", [128, N * F], _BF),
     "mb": ("sbuf", [128, F], _BF), "vb": ("sbuf", [128, F], _BF), "wb": ("sbuf", [128, F], _BF),
@@ -59,13 +60,14 @@ def _runs(ks):
 
 def rank_program(g, core, T, topo):
     rank = T.rank_of(core)
-    if rank is None:
-        return
     cores = list(T.cores)
     chips = []
     for c in cores:
         if topo.chip(c) not in chips:
             chips.append(topo.chip(c))
+    A = topo.chip(core)
+    if A not in chips:
+        return
     members = {ch: [c for c in cores if topo.chip(c) == ch] for ch in chips}
     W = 4 * F
 
@@ -75,27 +77,33 @@ def rank_program(g, core, T, topo):
     def direct(o, ch):
         return all(topo.may_write(o, d) for d in members[ch])
 
-    def handlers(ch):
-        free = list(members[ch])
+    def assign(ch, pool):
+        free = list(pool)
         h = {}
-
-        def cands(b):
-            return [c for c in members[ch] if direct(c, b)]
-        for b in sorted([b for b in chips if b != ch], key=lambda b: len(cands(b))):
-            c = [x for x in cands(b) if x in free][0]
+        for b in sorted([b for b in chips if b != ch], key=lambda b: len([c for c in pool if direct(c, b)])):
+            c = [x for x in free if direct(x, b)][0]
             h[b] = c
             free.remove(c)
+        return h, free
+
+    def handlers(ch):
+        h, free = assign(ch, members[ch])
         h[ch] = free[0]
         return h
 
-    A = topo.chip(core)
+    def xhandlers(ch):
+        pool = [c for c in range(SIMULATED) if topo.chip(c) == ch and c not in cores
+                and topo.die(c) != topo.die(members[ch][0])]
+        return assign(ch, pool)[0]
+
     ciA = chips.index(A)
     mem = members[A]
-    me = mem.index(core)
-    peers = [c for c in mem if c != core]
-    hA = handlers(A)
+    hA, xA = handlers(A), xhandlers(A)
     role = {c: b for b, c in hA.items()}
-    B = role[core]
+    xrole = {c: b for b, c in xA.items()}
+    if rank is None and core not in xrole:
+        return
+    B = role[core] if rank is not None else xrole[core]
     ciB = chips.index(B)
     sem = T.sem
     sy, sc, ve, pe = g.sync, g.scalar, g.vector, g.tensor
@@ -106,8 +114,113 @@ def rank_program(g, core, T, topo):
         rid, pid, _ = topo.addr(c)
         return DstId(rid=rid, pnc=pid)
 
-    targets = [mem[(me + j) % 4] for j in (1, 2, 3)]
-    order = [role[t] for t in targets] + [B]
+    def need_rest(dch):
+        ds = list(enumerate(members[dch]))
+        need = [x for x in ds if not all(direct(x[1], z) for z in chips if z != dch)]
+        return need, [x for x in ds if x not in need]
+
+    def s1_plan(src):
+        i = mem.index(src)
+        out = []
+        for j, ch in enumerate([role[mem[(i + d) % 4]] for d in (1, 2, 3, 0)]):
+            if ch == A:
+                parts = [(hA[A], (0, len(mem)))]
+            else:
+                nd, rs = need_rest(ch)
+                parts = [(hA[ch], _runs([k for k, d in nd])[0]), (xA[ch], _runs([k for k, d in rs])[0])]
+            parts = [p for p in parts if p[0] != src]
+            if not parts:
+                continue
+            full = topo.mask(src, parts[0][0])
+            for p in parts:
+                full &= topo.mask(src, p[0])
+            grp = full if j >= 2 else _take(full, _count(full) // 2, j)
+            n = _count(grp) // len(parts)
+            out.append((j, ch, [(d, run, _take(grp, n, x)) for x, (d, run) in enumerate(parts)]))
+        return out
+    s1_all = sum(_count(mk) for src in mem for j, ch, trs in s1_plan(src) for d, run, mk in trs if d == core)
+
+    def pieces(k):
+        ps_ = [T.land[:, s * W + k * F:s * W + (k + 1) * F] for s in range(len(mem)) if mem[s] != core]
+        if rank is not None:
+            ps_ = [T.grb[:, c0(B) + k * F:c0(B) + (k + 1) * F]] + ps_
+        return ps_
+
+    def s2_group(src, dch):
+        if topo.chip(src) == dch:
+            return [(k, d) for k, d in enumerate(members[dch]) if d != src]
+        nd, rs = need_rest(dch)
+        return nd if src in cores else rs
+
+    def s2_ne(src, gp):
+        n = _count(topo.mask(src, gp[0][1])) // len(gp)
+        while 128 % n:
+            n -= 1
+        return n
+
+    def s2_inc(b, dst):
+        dch = topo.chip(dst)
+        src = handlers(b)[dch]
+        if b != dch and dst not in [d for k, d in need_rest(dch)[0]]:
+            src = xhandlers(b)[dch]
+        return s2_ne(src, s2_group(src, dch))
+
+    def fold():
+        gp = s2_group(core, B)
+        ne = s2_ne(core, gp)
+        trs = []
+        for k, d in gp:
+            trs.append(RemoteDMATransfer(dst_ids=[did(d)], dma_engine_mask=_take(topo.mask(core, d), ne, len(trs)),
+                                         remote_sem=sem["p%d" % ciA], srcs=pieces(k),
+                                         dsts=[T.part[:, ciA * F:(ciA + 1) * F]], alu_op=1))
+            sent[0] += ne
+        g.remote_dma_fused(trs, local_sem=sem.sent)
+
+    def spread(ap, dsts, rsem):
+        mk = topo.mask(core, dsts[0])
+        for d in dsts:
+            mk &= topo.mask(core, d)
+        g.remote_dma_fused([RemoteDMATransfer(dst_ids=[did(d) for d in dsts], dma_engine_mask=mk, remote_sem=rsem,
+                                              srcs=[ap], dsts=[ap for d in dsts], alu_op=0)], local_sem=sem.sent)
+        sent[0] += _count(mk)
+
+    def cols(ch, run):
+        return slice(c0(ch) + run[0] * F, c0(ch) + run[1] * F)
+
+    def dset(x, y):
+        d = [k for k, o in enumerate(members[x]) if direct(o, y)]
+        return d, [k for k in range(len(members[x])) if k not in d]
+
+    on_n = _count(topo.mask(core, [c for c in mem if c != core][0]))
+
+    def off_mask(c):
+        mk = topo.mask(c, [p for p in mem if p != c][0])
+        for z in chips:
+            if z != A and direct(c, z):
+                mk &= topo.mask(c, handlers(z)[A])
+        return mk
+
+    def relays_of(c):
+        return [xA[z] for z in chips if z != A and not direct(c, z)]
+
+    def g1_n(k):
+        return on_n // 2 if relays_of(mem[k]) else on_n - _count(off_mask(mem[k]))
+
+    if rank is None:
+        g.wait_ge(sem.s1, s1_all)
+        fold()
+        rel = dset(A, B)[1]
+        for k in rel:
+            g.wait_ge(sem["q%d" % k], g1_n(k))
+        for run in _runs(rel):
+            spread(T.yb[:, cols(A, run)], [handlers(B)[A]], sem["f%d" % ciA])
+        g.wait_ge(sem.sent, sent[0])
+        return
+
+    me = mem.index(core)
+    peers = [c for c in mem if c != core]
+
+    order = [role[mem[(me + d) % 4]] for d in (1, 2, 3, 0)]
     for j, ch in enumerate(order):
         q = sy if j % 2 == 0 else sc
         q.dma_start(T.grb[:, c0(ch):c0(ch) + W], T.gr[:, c0(ch):c0(ch) + W]).then_inc(sem["l%d" % j], 16)
@@ -122,52 +235,17 @@ def rank_program(g, core, T, topo):
     ve.tensor_scalar(T.i75[:], T.idn[:], B1, None, OP.mult).then_inc(sem.c_i75, 1)
     ve.tensor_scalar(T.i25[:], T.idn[:], 1.0 - B1, None, OP.mult).then_inc(sem.c_i25, 1)
 
-    def s1_mask(src, dst):
-        j = (mem.index(dst) - mem.index(src) - 1) % 4
-        full = topo.mask(src, dst)
-        return full if j == 2 else _take(full, _count(full) // 2, j)
-    for j, t in enumerate(targets):
-        ch = role[t]
-        slot = [c for c in mem if c != t].index(core)
-        rid, pid, _ = topo.addr(t)
-        mk = s1_mask(core, t)
+    for j, ch, trs in s1_plan(core):
         g.wait_ge(sem["l%d" % j], 16)
-        g.remote_dma(T.land[:, slot * W:(slot + 1) * W], T.grb[:, c0(ch):c0(ch) + W], sem.s1, sem.sent, pid, rid, mk)
-        sent[0] += _count(mk)
-    s1_all = sum(_count(s1_mask(p, core)) for p in peers)
+        g.remote_dma_fused([RemoteDMATransfer(dst_ids=[did(d)], dma_engine_mask=mk, remote_sem=sem.s1,
+                                              srcs=[T.grb[:, c0(ch) + r[0] * F:c0(ch) + r[1] * F]],
+                                              dsts=[T.land[:, me * W + r[0] * F:me * W + r[1] * F]], alu_op=0)
+                            for d, r, mk in trs], local_sem=sem.sent)
+        sent[0] += sum(_count(mk) for d, r, mk in trs)
 
-    def pieces(k):
-        return [T.grb[:, c0(B) + k * F:c0(B) + (k + 1) * F]] + [T.land[:, s * W + k * F:s * W + (k + 1) * F] for s in range(3)]
-
-    def s2_groups(src, dch):
-        ds = [(k, d) for k, d in enumerate(members[dch]) if d != src]
-        if topo.chip(src) == dch:
-            return [ds]
-        need = [x for x in ds if not all(direct(x[1], z) for z in chips if z != dch)]
-        rest = [x for x in ds if x not in need]
-        return [gp for gp in (need, rest) if gp]
-
-    def s2_ne(src, gp):
-        n = _count(topo.mask(src, gp[0][1])) // len(gp)
-        while 128 % n:
-            n -= 1
-        return n
-
-    def s2_inc(src, dst):
-        for gp in s2_groups(src, topo.chip(dst)):
-            if dst in [d for k, d in gp]:
-                return s2_ne(src, gp)
     g.wait_ge(sem.l3, 16)
     g.wait_ge(sem.s1, s1_all)
-    for gp in s2_groups(core, B):
-        ne = s2_ne(core, gp)
-        trs = []
-        for k, d in gp:
-            trs.append(RemoteDMATransfer(dst_ids=[did(d)], dma_engine_mask=_take(topo.mask(core, d), ne, len(trs)),
-                                         remote_sem=sem["p%d" % ciA], srcs=pieces(k),
-                                         dsts=[T.part[:, ciA * F:(ciA + 1) * F]], alu_op=1))
-            sent[0] += ne
-        g.remote_dma_fused(trs, local_sem=sem.sent)
+    fold()
 
     sc.wait_ge(sem.lv, 16)
     sc.activation(T.ra[:], T.vb[:], AF.Sqrt, bias=TINY, scale=B2).then_inc(sem.c_ra, 1)
@@ -187,11 +265,11 @@ def rank_program(g, core, T, topo):
         for r in raw[1:]:
             todo.append((sem.s1, s1_all, r))
     else:
-        todo.append((sem["p%d" % ciA], s2_inc(hA[A], core), T.part[:, ciA * F:(ciA + 1) * F]))
+        todo.append((sem["p%d" % ciA], s2_inc(A, core), T.part[:, ciA * F:(ciA + 1) * F]))
     away = sorted([b for b in chips if b != A], key=lambda b: 0 if topo.same_plane(A, b) else 1)
     for b in away:
         ci = chips.index(b)
-        todo.append((sem["p%d" % ci], s2_inc(handlers(b)[A], core), T.part[:, ci * F:(ci + 1) * F]))
+        todo.append((sem["p%d" % ci], s2_inc(b, core), T.part[:, ci * F:(ci + 1) * F]))
     pe.wait_ge(sem.c_idn, 1)
     pe.wait_ge(sem.c_i75, 1)
     pe.wait_ge(sem.c_i25, 1)
@@ -239,63 +317,35 @@ def rank_program(g, core, T, topo):
     sc.wait_ge(sem.c_mo, 1)
     sc.dma_start(T.mo[:], T.mob[:]).then_inc(sem.tm, 16)
 
-    def spread(ap, dsts, rsem):
-        mk = topo.mask(core, dsts[0])
-        for d in dsts:
-            mk &= topo.mask(core, d)
-        g.remote_dma_fused([RemoteDMATransfer(dst_ids=[did(d) for d in dsts], dma_engine_mask=mk, remote_sem=rsem,
-                                              srcs=[ap], dsts=[ap for d in dsts], alu_op=0)], local_sem=sem.sent)
-        sent[0] += _count(mk)
-
-    def cols(ch, run):
-        return slice(c0(ch) + run[0] * F, c0(ch) + run[1] * F)
-
-    def dset(x, y):
-        d = [k for k, o in enumerate(members[x]) if direct(o, y)]
-        return d, [k for k in range(len(members[x])) if k not in d]
-
-    on_n = _count(topo.mask(core, peers[0]))
-
-    def off_mask(c):
-        mk = topo.mask(c, [p for p in mem if p != c][0])
-        for z in chips:
-            if z != A and direct(c, z):
-                mk &= topo.mask(c, handlers(z)[A])
-        return mk
-
-    def duty(c):
-        return role[c] != A and len(dset(A, role[c])[1]) > 0
-
-    def g1_n(k):
-        return on_n - _count(off_mask(mem[k])) if duty(mem[k]) else on_n
     far_dsts = [handlers(z)[A] for z in chips if z != A and direct(core, z)]
+    full = topo.mask(core, peers[0])
     g.wait_ge(sem.c_w, 1)
-    if duty(core):
+    if relays_of(core):
+        grp = [(relays_of(core), _take(full, on_n // 2, 0)), (peers, _take(full, on_n // 2, 1))]
+        g.remote_dma_fused([RemoteDMATransfer(dst_ids=[did(d) for d in ds], dma_engine_mask=mk,
+                                              remote_sem=sem["q%d" % me], srcs=[own], dsts=[own for d in ds], alu_op=0)
+                            for ds, mk in grp], local_sem=sem.sent)
+        sent[0] += on_n
+        spread(own, far_dsts, sem["e%d" % ciA])
+    else:
         mo_ = off_mask(core)
-        mi_ = topo.mask(core, peers[0]) & ~mo_
+        mi_ = full & ~mo_
         g.remote_dma_fused([
             RemoteDMATransfer(dst_ids=[did(d) for d in far_dsts], dma_engine_mask=mo_, remote_sem=sem["e%d" % ciA],
                               srcs=[own], dsts=[own for d in far_dsts], alu_op=0),
             RemoteDMATransfer(dst_ids=[did(d) for d in peers], dma_engine_mask=mi_, remote_sem=sem["q%d" % me],
                               srcs=[own], dsts=[own for d in peers], alu_op=0)], local_sem=sem.sent)
         sent[0] += _count(mo_) + _count(mi_)
-    else:
-        spread(own, peers, sem["q%d" % me])
-        spread(own, far_dsts, sem["e%d" % ciA])
+
+    def off_n(b):
+        return _count(topo.mask(handlers(b)[A], core))
     if B != A:
-        partner = handlers(B)[A]
-        off_n = _count(topo.mask(partner, core))
-        rel = dset(A, B)[1]
-        for k in rel:
-            g.wait_ge(sem["q%d" % k], g1_n(k))
-        for run in _runs(rel):
-            spread(T.yb[:, cols(A, run)], [partner], sem["f%d" % ciA])
         dB, rB = dset(B, A)
-        g.wait_ge(sem["e%d" % ciB], off_n * len(dB))
+        g.wait_ge(sem["e%d" % ciB], off_n(B) * len(dB))
         for run in _runs(dB):
             spread(T.yb[:, cols(B, run)], peers, sem["e%d" % ciB])
         if rB:
-            g.wait_ge(sem["f%d" % ciB], off_n * len(_runs(rB)))
+            g.wait_ge(sem["f%d" % ciB], off_n(B) * len(_runs(rB)))
             for run in _runs(rB):
                 spread(T.yb[:, cols(B, run)], peers, sem["f%d" % ciB])
 
@@ -308,7 +358,7 @@ def rank_program(g, core, T, topo):
             if not ks:
                 continue
             if b == B:
-                n = _count(topo.mask(handlers(b)[A], core)) * (len(ks) if part == 0 else len(_runs(ks)))
+                n = off_n(b) * (len(ks) if part == 0 else len(_runs(ks)))
             else:
                 n = on_n * len(_runs(ks))
             for run in _runs(ks):

import math
from concourse.bass import DstId, RemoteDMATransfer
from concourse.mybir import AluOpType, ActivationFunctionType

N = 16
F = 128
SIMULATED = 112
B1, B2, LR, EPS = 0.75, 0.875, 2.0, 0.001
TINY = 1e-12

_BF = "bfloat16"
_FP = "float32"
SCRATCH = {
    "grb": ("sbuf", [128, N * F], _BF),
    "land": ("sbuf", [128, 4 * 4 * F], _BF),
    "part": ("sbuf", [128, 4 * F], _BF),
    "yb": ("sbuf", [128, N * F], _BF),
    "mb": ("sbuf", [128, F], _BF), "vb": ("sbuf", [128, F], _BF), "wb": ("sbuf", [128, F], _BF),
    "ones": ("sbuf", [128, F], _BF), "idn": ("sbuf", [128, F], _BF),
    "i25": ("sbuf", [128, F], _BF), "i75": ("sbuf", [128, F], _BF),
    "ra": ("sbuf", [128, F], _FP), "ira": ("sbuf", [128, F], _FP), "ia": ("sbuf", [128, F], _FP),
    "e2": ("sbuf", [128, F], _FP), "n2": ("sbuf", [128, F], _FP), "av": ("sbuf", [128, F], _FP),
    "dd": ("sbuf", [128, F], _FP), "rec": ("sbuf", [128, F], _FP),
    "mob": ("sbuf", [128, F], _BF), "vob": ("sbuf", [128, F], _BF),
    "ps": ("psum", [128, 512], _FP), "pm": ("psum", [128, 512], _FP), "psq": ("psum", [128, 512], _FP),
    "px": ("psum", [128, 512], _FP), "ph": ("psum", [128, 512], _FP), "pu": ("psum", [128, 512], _FP),
    "pt": ("psum", [128, 512], _FP),
}
SEMAPHORES = (["l0", "l1", "l2", "l3", "lm", "lv", "lw", "s1", "sent"]
              + ["p%d" % i for i in range(4)] + ["q%d" % i for i in range(4)] + ["e%d" % i for i in range(4)]
              + ["f%d" % i for i in range(4)] + ["t%d" % i for i in range(8)]
              + ["tm", "tv", "c_ones", "c_idn", "c_i25", "c_i75", "c_ra", "c_ira", "c_ia", "c_e2", "c_n2", "c_av",
                 "c_s", "c_m", "c_sq", "c_x", "c_h", "c_um", "c_d", "c_rec", "c_t", "c_w", "c_vo", "c_mo"])


def _bits(mask):
    return [b for b in range(16) if (mask >> b) & 1]


def _take(mask, n, i=0):
    m = 0
    for b in _bits(mask)[i * n:(i + 1) * n]:
        m |= 1 << b
    return m


def _count(mask):
    return len(_bits(mask))


def _runs(ks):
    out = []
    for k in sorted(ks):
        if out and out[-1][1] == k:
            out[-1] = (out[-1][0], k + 1)
        else:
            out.append((k, k + 1))
    return out


def rank_program(g, core, T, topo):
    rank = T.rank_of(core)
    cores = list(T.cores)
    chips = []
    for c in cores:
        if topo.chip(c) not in chips:
            chips.append(topo.chip(c))
    A = topo.chip(core)
    if A not in chips:
        return
    members = {ch: [c for c in cores if topo.chip(c) == ch] for ch in chips}
    W = 4 * F

    def c0(ch):
        return T.rank_of(members[ch][0]) * F

    def direct(o, ch):
        return all(topo.may_write(o, d) for d in members[ch])

    def assign(ch, pool):
        free = list(pool)
        h = {}
        for b in sorted([b for b in chips if b != ch], key=lambda b: len([c for c in pool if direct(c, b)])):
            c = [x for x in free if direct(x, b)][0]
            h[b] = c
            free.remove(c)
        return h, free

    def handlers(ch):
        h, free = assign(ch, members[ch])
        h[ch] = free[0]
        return h

    def xhandlers(ch):
        pool = [c for c in range(SIMULATED) if topo.chip(c) == ch and c not in cores
                and topo.die(c) != topo.die(members[ch][0])]
        return assign(ch, pool)[0]

    ciA = chips.index(A)
    mem = members[A]
    hA, xA = handlers(A), xhandlers(A)
    role = {c: b for b, c in hA.items()}
    xrole = {c: b for b, c in xA.items()}
    if rank is None and core not in xrole:
        return
    B = role[core] if rank is not None else xrole[core]
    ciB = chips.index(B)
    sem = T.sem
    sy, sc, ve, pe = g.sync, g.scalar, g.vector, g.tensor
    AF, OP = ActivationFunctionType, AluOpType
    sent = [0]

    def did(c):
        rid, pid, _ = topo.addr(c)
        return DstId(rid=rid, pnc=pid)

    def need_rest(dch):
        ds = list(enumerate(members[dch]))
        need = [x for x in ds if not all(direct(x[1], z) for z in chips if z != dch)]
        return need, [x for x in ds if x not in need]

    def s1_plan(src):
        i = mem.index(src)
        out = []
        for j, ch in enumerate([role[mem[(i + d) % 4]] for d in (1, 2, 3, 0)]):
            if ch == A:
                parts = [(hA[A], (0, len(mem)))]
            else:
                nd, rs = need_rest(ch)
                parts = [(hA[ch], _runs([k for k, d in nd])[0]), (xA[ch], _runs([k for k, d in rs])[0])]
            parts = [p for p in parts if p[0] != src]
            if not parts:
                continue
            full = topo.mask(src, parts[0][0])
            for p in parts:
                full &= topo.mask(src, p[0])
            grp = full if j >= 2 else _take(full, _count(full) // 2, j)
            n = _count(grp) // len(parts)
            out.append((j, ch, [(d, run, _take(grp, n, x)) for x, (d, run) in enumerate(parts)]))
        return out
    s1_all = sum(_count(mk) for src in mem for j, ch, trs in s1_plan(src) for d, run, mk in trs if d == core)

    def pieces(k):
        ps_ = [T.land[:, s * W + k * F:s * W + (k + 1) * F] for s in range(len(mem)) if mem[s] != core]
        if rank is not None:
            ps_ = [T.grb[:, c0(B) + k * F:c0(B) + (k + 1) * F]] + ps_
        return ps_

    def s2_group(src, dch):
        if topo.chip(src) == dch:
            return [(k, d) for k, d in enumerate(members[dch]) if d != src]
        nd, rs = need_rest(dch)
        return nd if src in cores else rs

    def s2_ne(src, gp):
        n = _count(topo.mask(src, gp[0][1])) // len(gp)
        while 128 % n:
            n -= 1
        return n

    def s2_inc(b, dst):
        dch = topo.chip(dst)
        src = handlers(b)[dch]
        if b != dch and dst not in [d for k, d in need_rest(dch)[0]]:
            src = xhandlers(b)[dch]
        return s2_ne(src, s2_group(src, dch))

    def fold():
        gp = s2_group(core, B)
        ne = s2_ne(core, gp)
        trs = []
        for k, d in gp:
            trs.append(RemoteDMATransfer(dst_ids=[did(d)], dma_engine_mask=_take(topo.mask(core, d), ne, len(trs)),
                                         remote_sem=sem["p%d" % ciA], srcs=pieces(k),
                                         dsts=[T.part[:, ciA * F:(ciA + 1) * F]], alu_op=1))
            sent[0] += ne
        g.remote_dma_fused(trs, local_sem=sem.sent)

    def spread(ap, dsts, rsem):
        mk = topo.mask(core, dsts[0])
        for d in dsts:
            mk &= topo.mask(core, d)
        g.remote_dma_fused([RemoteDMATransfer(dst_ids=[did(d) for d in dsts], dma_engine_mask=mk, remote_sem=rsem,
                                              srcs=[ap], dsts=[ap for d in dsts], alu_op=0)], local_sem=sem.sent)
        sent[0] += _count(mk)

    def cols(ch, run):
        return slice(c0(ch) + run[0] * F, c0(ch) + run[1] * F)

    def dset(x, y):
        d = [k for k, o in enumerate(members[x]) if direct(o, y)]
        return d, [k for k in range(len(members[x])) if k not in d]

    on_n = _count(topo.mask(core, [c for c in mem if c != core][0]))

    def off_mask(c):
        mk = topo.mask(c, [p for p in mem if p != c][0])
        for z in chips:
            if z != A and direct(c, z):
                mk &= topo.mask(c, handlers(z)[A])
        return mk

    def relays_of(c):
        return [xA[z] for z in chips if z != A and not direct(c, z)]

    def g1_n(k):
        return on_n // 2 if relays_of(mem[k]) else on_n - _count(off_mask(mem[k]))

    if rank is None:
        g.wait_ge(sem.s1, s1_all)
        fold()
        rel = dset(A, B)[1]
        for k in rel:
            g.wait_ge(sem["q%d" % k], g1_n(k))
        for run in _runs(rel):
            spread(T.yb[:, cols(A, run)], [handlers(B)[A]], sem["f%d" % ciA])
        g.wait_ge(sem.sent, sent[0])
        return

    me = mem.index(core)
    peers = [c for c in mem if c != core]

    order = [role[mem[(me + d) % 4]] for d in (1, 2, 3, 0)]
    for j, ch in enumerate(order):
        q = sy if j % 2 == 0 else sc
        q.dma_start(T.grb[:, c0(ch):c0(ch) + W], T.gr[:, c0(ch):c0(ch) + W]).then_inc(sem["l%d" % j], 16)
    sc.dma_start(T.vb[:], T.v[:]).then_inc(sem.lv, 16)
    sy.dma_start(T.mb[:], T.m[:]).then_inc(sem.lm, 16)
    sy.dma_start(T.wb[:], T.w[:]).then_inc(sem.lw, 16)

    ve.memset(T.ones[:], 1.0).then_inc(sem.c_ones, 1)
    g.wait_ge(sem.c_ones, 1)
    g.affine_select(T.idn[:], T.ones[:], [[-1, F]], OP.is_equal, 0.0, 0, 1).then_inc(sem.c_idn, 1)
    ve.wait_ge(sem.c_idn, 1)
    ve.tensor_scalar(T.i75[:], T.idn[:], B1, None, OP.mult).then_inc(sem.c_i75, 1)
    ve.tensor_scalar(T.i25[:], T.idn[:], 1.0 - B1, None, OP.mult).then_inc(sem.c_i25, 1)

    for j, ch, trs in s1_plan(core):
        g.wait_ge(sem["l%d" % j], 16)
        g.remote_dma_fused([RemoteDMATransfer(dst_ids=[did(d)], dma_engine_mask=mk, remote_sem=sem.s1,
                                              srcs=[T.grb[:, c0(ch) + r[0] * F:c0(ch) + r[1] * F]],
                                              dsts=[T.land[:, me * W + r[0] * F:me * W + r[1] * F]], alu_op=0)
                            for d, r, mk in trs], local_sem=sem.sent)
        sent[0] += sum(_count(mk) for d, r, mk in trs)

    g.wait_ge(sem.l3, 16)
    g.wait_ge(sem.s1, s1_all)
    fold()

    sc.wait_ge(sem.lv, 16)
    sc.activation(T.ra[:], T.vb[:], AF.Sqrt, bias=TINY, scale=B2).then_inc(sem.c_ra, 1)
    sc.activation(T.av[:], T.vb[:], AF.Copy, scale=B2).then_inc(sem.c_av, 1)
    ve.wait_ge(sem.c_ra, 1)
    ve.reciprocal(T.ira[:], T.ra[:]).then_inc(sem.c_ira, 1)
    ve.wait_ge(sem.c_ira, 1)
    ve.tensor_tensor(T.ia[:], T.ira[:], T.ira[:], OP.mult).then_inc(sem.c_ia, 1)
    ve.tensor_scalar(T.e2[:], T.ira[:], EPS, None, OP.mult).then_inc(sem.c_e2, 1)
    ve.tensor_scalar(T.n2[:], T.ira[:], -LR, None, OP.mult).then_inc(sem.c_n2, 1)

    ps, pm = T.ps[:, 0:F], T.pm[:, 0:F]
    todo = []
    if B == A:
        raw = pieces(me)
        todo.append((sem.l3, 16, raw[0]))
        for r in raw[1:]:
            todo.append((sem.s1, s1_all, r))
    else:
        todo.append((sem["p%d" % ciA], s2_inc(A, core), T.part[:, ciA * F:(ciA + 1) * F]))
    away = sorted([b for b in chips if b != A], key=lambda b: 0 if topo.same_plane(A, b) else 1)
    for b in away:
        ci = chips.index(b)
        todo.append((sem["p%d" % ci], s2_inc(b, core), T.part[:, ci * F:(ci + 1) * F]))
    pe.wait_ge(sem.c_idn, 1)
    pe.wait_ge(sem.c_i75, 1)
    pe.wait_ge(sem.c_i25, 1)
    pe.wait_ge(sem.lm, 16)
    pe.matmul(pm, T.i75[:], T.mb[:], True, False)
    for i, (s, n, ap) in enumerate(todo):
        last = i == len(todo) - 1
        pe.wait_ge(s, n)
        a = pe.matmul(ps, T.idn[:], ap, i == 0, last)
        if last:
            a.then_inc(sem.c_s, 1)
        b_ = pe.matmul(pm, T.i25[:], ap, False, last)
        if last:
            b_.then_inc(sem.c_m, 1)

    own = T.yb[:, rank * F:(rank + 1) * F]
    psq, px, ph, pu, pt = T.psq[:, 0:F], T.px[:, 0:F], T.ph[:, 0:F], T.pu[:, 0:F], T.pt[:, 0:F]
    sc.wait_ge(sem.c_s, 1)
    sc.activation(psq, ps, AF.Square, scale=math.sqrt(1.0 - B2)).then_inc(sem.c_sq, 1)
    ve.wait_ge(sem.c_ia, 1)
    ve.wait_ge(sem.c_sq, 1)
    ve.tensor_tensor(px, psq, T.ia[:], OP.mult).then_inc(sem.c_x, 1)
    sc.wait_ge(sem.c_x, 1)
    sc.activation(ph, px, AF.Sqrt, bias=1.0, scale=1.0).then_inc(sem.c_h, 1)
    ve.wait_ge(sem.c_n2, 1)
    ve.wait_ge(sem.c_m, 1)
    ve.tensor_tensor(pu, pm, T.n2[:], OP.mult).then_inc(sem.c_um, 1)
    ve.wait_ge(sem.c_e2, 1)
    ve.wait_ge(sem.c_h, 1)
    ve.tensor_tensor(T.dd[:], ph, T.e2[:], OP.add).then_inc(sem.c_d, 1)
    ve.wait_ge(sem.c_d, 1)
    ve.reciprocal(T.rec[:], T.dd[:]).then_inc(sem.c_rec, 1)
    ve.wait_ge(sem.c_rec, 1)
    ve.wait_ge(sem.c_um, 1)
    ve.tensor_tensor(pt, pu, T.rec[:], OP.mult).then_inc(sem.c_t, 1)
    ve.wait_ge(sem.c_t, 1)
    ve.wait_ge(sem.lw, 16)
    ve.tensor_tensor(own, pt, T.wb[:], OP.add).then_inc(sem.c_w, 1)
    ve.wait_ge(sem.c_av, 1)
    ve.tensor_tensor(T.vob[:], psq, T.av[:], OP.add).then_inc(sem.c_vo, 1)
    sc.wait_ge(sem.c_um, 1)
    sc.activation(T.mob[:], pm, AF.Copy).then_inc(sem.c_mo, 1)
    sy.wait_ge(sem.c_vo, 1)
    sy.dma_start(T.vo[:], T.vob[:]).then_inc(sem.tv, 16)
    sc.wait_ge(sem.c_mo, 1)
    sc.dma_start(T.mo[:], T.mob[:]).then_inc(sem.tm, 16)

    far_dsts = [handlers(z)[A] for z in chips if z != A and direct(core, z)]
    full = topo.mask(core, peers[0])
    g.wait_ge(sem.c_w, 1)
    if relays_of(core):
        grp = [(relays_of(core), _take(full, on_n // 2, 0)), (peers, _take(full, on_n // 2, 1))]
        g.remote_dma_fused([RemoteDMATransfer(dst_ids=[did(d) for d in ds], dma_engine_mask=mk,
                                              remote_sem=sem["q%d" % me], srcs=[own], dsts=[own for d in ds], alu_op=0)
                            for ds, mk in grp], local_sem=sem.sent)
        sent[0] += on_n
        spread(own, far_dsts, sem["e%d" % ciA])
    else:
        mo_ = off_mask(core)
        mi_ = full & ~mo_
        g.remote_dma_fused([
            RemoteDMATransfer(dst_ids=[did(d) for d in far_dsts], dma_engine_mask=mo_, remote_sem=sem["e%d" % ciA],
                              srcs=[own], dsts=[own for d in far_dsts], alu_op=0),
            RemoteDMATransfer(dst_ids=[did(d) for d in peers], dma_engine_mask=mi_, remote_sem=sem["q%d" % me],
                              srcs=[own], dsts=[own for d in peers], alu_op=0)], local_sem=sem.sent)
        sent[0] += _count(mo_) + _count(mi_)

    def off_n(b):
        return _count(topo.mask(handlers(b)[A], core))
    if B != A:
        dB, rB = dset(B, A)
        g.wait_ge(sem["e%d" % ciB], off_n(B) * len(dB))
        for run in _runs(dB):
            spread(T.yb[:, cols(B, run)], peers, sem["e%d" % ciB])
        if rB:
            g.wait_ge(sem["f%d" % ciB], off_n(B) * len(_runs(rB)))
            for run in _runs(rB):
                spread(T.yb[:, cols(B, run)], peers, sem["f%d" % ciB])

    jobs = [([(sem.c_w, 1)] + [(sem["q%d" % k], g1_n(k)) for k in range(4) if k != me], slice(c0(A), c0(A) + W))]
    first = ([B] if B != A else []) + [b for b in away if b != B]
    for part in (0, 1):
        for b in first:
            ci = chips.index(b)
            ks = dset(b, A)[part]
            if not ks:
                continue
            if b == B:
                n = off_n(b) * (len(ks) if part == 0 else len(_runs(ks)))
            else:
                n = on_n * len(_runs(ks))
            for run in _runs(ks):
                jobs.append(([(sem[("e%d" if part == 0 else "f%d") % ci], n)], cols(b, run)))
    for i, (ws, cs) in enumerate(jobs):
        q = sy if i % 2 == 0 else sc
        for s, n in ws:
            q.wait_ge(s, n)
        q.dma_start(T.y[:, cs], T.yb[:, cs]).then_inc(sem["t%d" % i], 16)

    g.wait_ge(sem.sent, sent[0])
    g.wait_ge(sem.tm, 16)
    g.wait_ge(sem.tv, 16)
    for i in range(len(jobs)):
        g.wait_ge(sem["t%d" % i], 16)
